import numpy as np, ml_dtypes
CORES = [22,46,70,150,174,198,278,302,326,406,430,454]
N = 12
import mx_ref
NC, G = 128, 2
EPS = 0.001
BF = ml_dtypes.bfloat16
def cut(t, i, w=512):
    return t[:, w * i:w * i + w]
def tile(rs):
    return np.stack(rs, axis=2).reshape(128, -1).astype(BF)
def layer(w, X):
    out = []
    for i in range(G):
        for t in range(len(X)):
            p = mx_ref.matmul(mx_ref.quantize(cut(w, len(X) * i + t)), X[t])
            z = p if t == 0 else z + p
        out.append(z)
    return out
def normed(Z, s):
    return [np.maximum(k * z, 0) * f for z, f in zip(Z, s) for k in (1, -1)]
def setup_inputs(rng):
    def f(*shape):
        return mx_ref.flush((rng.standard_normal(shape, dtype=np.float32) * np.exp2(rng.integers(-2, 3, shape[:-1] + (1,)))).astype(BF))
    return {"x": f(N, 128, 4 * NC), "w1": f(N, 128, G * 512), "w2": f(N, 128, 2 * 512)}
def setup_inputs_blocks(rng):
    d = setup_inputs(rng)
    for k in ("x", "w1", "w2"): d[k] = mx_ref.spread(d[k], rng, 4)
    return d
def setup_inputs_wide(rng):
    d = setup_inputs(rng)
    for k in ("x", "w1", "w2"): d[k] = mx_ref.flush((d[k].astype(np.float32) * np.exp2(rng.integers(-5, 6, (N, 1, 1))).astype(np.float32)).astype(BF))
    return d
def setup_inputs_rows(rng):
    d = setup_inputs(rng); v = d["w1"].astype(np.float32).reshape(N, 128, -1, 4)
    d["w1"] = mx_ref.flush((v * np.exp2(rng.integers(-6, 7, (N, 1, v.shape[2], 1))).astype(np.float32)).reshape(d["w1"].shape).astype(BF))
    return d
def setup_inputs_faint(rng):
    d = setup_inputs(rng); d["x"] = mx_ref.flush((d["x"].astype(np.float32) * np.float32(2.0 ** -12)).astype(BF))
    return d
def reference(x, w1, w2, own=None):
    Z = [layer(w1[r], [mx_ref.quantize(x[r])]) for r in range(N)]
    ms = [sum((Z[r][i].astype(np.float64) ** 2).sum(axis=1, keepdims=True) for r in range(N)) / (N * NC) for i in range(G)]
    s = [(1 / np.sqrt(m + EPS)).astype(np.float32) for m in ms]
    h = np.stack([tile(normed(Z[r], s)) for r in range(N)])
    use = h if own is None else own["h"]
    H = [mx_ref.quantize(use[j]) for j in range(N)]
    y = np.zeros((N, 128, NC), np.float32)
    for r in range(N):
        y[r] = mx_ref.matmul(mx_ref.quantize(cut(w2[r], 0)), H[r]) + mx_ref.matmul(mx_ref.quantize(cut(w2[r], 1)), H[(r + 1) % N])
    return {"h": h, "y": y}

@@ -1,0 +1,193 @@
+from concourse.bass import DstId, RemoteDMATransfer
+from concourse.mybir import dt, AluOpType, AxisListType, ActivationFunctionType
+
+NC = 128
+EPS = 0.001
+
+SCRATCH = {
+    "xb": ("sbuf", [128, 512], "bfloat16"),
+    "w1b": ("sbuf", [128, 1024], "bfloat16"),
+    "w2b": ("sbuf", [128, 1024], "bfloat16"),
+    "xq": ("sbuf", [128, 128], "float8_e4m3fn_x4"), "xs": ("sbuf", [128, 128], "uint8"),
+    "w1q": ("sbuf", [128, 256], "float8_e4m3fn_x4"), "w1s": ("sbuf", [128, 256], "uint8"),
+    "w2q": ("sbuf", [128, 256], "float8_e4m3fn_x4"), "w2s": ("sbuf", [128, 256], "uint8"),
+    "hq": ("sbuf", [128, 128], "float8_e4m3fn_x4"), "hs": ("sbuf", [128, 128], "uint8"),
+    "nq": ("sbuf", [128, 128], "float8_e4m3fn_x4"), "ns": ("sbuf", [128, 128], "uint8"),
+    "z": ("psum", [128, 1024], "float32"),
+    "yp": ("psum", [128, 512], "float32"),
+    "sqj": ("sbuf", [128, 256], "float32"),
+    "j1": ("sbuf", [128, 4], "float32"), "j2": ("sbuf", [128, 4], "float32"),
+    "l1": ("sbuf", [128, 12], "float32"),
+    "l2": ("sbuf", [128, 16], "float32"),
+    "tot": ("sbuf", [128, 2], "float32"),
+    "vv": ("sbuf", [128, 2], "float32"), "rv": ("sbuf", [128, 2], "float32"), "rt": ("sbuf", [128, 2], "float32"),
+    "sf": ("sbuf", [128, 1], "float32"),
+    "pz": ("sbuf", [128, 512], "float32"),
+    "ht": ("sbuf", [128, 512], "bfloat16"),
+    "yb": ("sbuf", [128, 128], "float32"),
+}
+SEMAPHORES = ["lx", "la", "lb", "lw", "qx", "qa", "qb", "qw", "m0", "m1", "s0", "s1", "pv", "ps", "a1", "r0", "r1", "a2",
+              "t0", "t1", "rs", "vs", "rc", "sc", "hv", "hc", "qh", "ah", "my", "yc", "sh", "sy", "out", "ho"]
+
+
+def _plan(cores, topo):
+    racks = {}
+    for c in cores:
+        racks.setdefault(topo.rack(topo.host(c)), {}).setdefault(topo.host(c), []).append(c)
+    groups = []
+    for rk in sorted(racks):
+        a, b = [racks[rk][h] for h in sorted(racks[rk])]
+        k = (len(a) + 1) // 2
+        groups.append(a[:k] + b[:len(b) - k])
+        groups.append(a[k:] + b[len(b) - k:])
+    fan = {c: [] for c in cores}
+    for gr in groups:
+        rec = [v for v in cores if v not in gr]
+        rec.sort(key=lambda v: sum(1 for u in gr if topo.may_write(u, v)))
+        for v in rec:
+            opts = [u for u in gr if topo.may_write(u, v)]
+            fan[min(opts, key=lambda u: (len(fan[u]), topo.chip(u) != topo.chip(v)))].append(v)
+    return groups, fan
+
+
+def _mask(topo, src, dsts):
+    m = topo.mask(src, dsts[0])
+    for d in dsts[1:]:
+        m &= topo.mask(src, d)
+    return m
+
+
+def _engines(m):
+    return bin(m).count("1")
+
+
+def _spread(g, topo, core, dsts, ap, remote_sem, local_sem):
+    ids = []
+    for d in dsts:
+        rid, pid = topo.addr(d, core)
+        ids.append(DstId(rid=rid, pnc=pid))
+    g.remote_dma_fused([RemoteDMATransfer(dst_ids=ids, dma_engine_mask=_mask(topo, core, dsts), remote_sem=remote_sem,
+                                          srcs=[ap], dsts=[ap for _ in dsts], alu_op=0)], local_sem=local_sem)
+
+
+def rank_program(g, core, T, topo):
+    rank = T.rank_of(core)
+    if rank is None:
+        return
+    cores = [int(c) for c in T.cores]
+    n = len(cores)
+    groups, fan = _plan(cores, topo)
+    t = [i for i, gr in enumerate(groups) if core in gr][0]
+    q = groups[t].index(core)
+    peers = [u for u in groups[t] if u != core]
+    in1 = sum(_engines(_mask(topo, u, [w for w in groups[t] if w != u])) for u in peers)
+    in2 = sum(_engines(_mask(topo, u, fan[u])) for u in cores if core in fan[u])
+    S, A, OP = T.sem, ActivationFunctionType, AluOpType
+    V, SC, PE, SY = g.vector, g.scalar, g.tensor, g.sync
+    inv = 1.0 / (n * NC)
+    mine1, mine2 = T.l1[:, 4 * q:4 * q + 2], T.l2[:, 4 * t:4 * t + 2]
+    e1 = len(groups[t]) * 4
+    e2 = len(groups) * 4
+
+    SY.dma_start(T.xb[:], T.x[:]).then_inc(S.lx, 16)
+    SC.dma_start(T.w1b[:, 0:512], T.w1[:, 0:512]).then_inc(S.la, 16)
+    SY.dma_start(T.w1b[:, 512:1024], T.w1[:, 512:1024]).then_inc(S.lb, 16)
+    SY.dma_start(T.w2b[:], T.w2[:]).then_inc(S.lw, 16)
+
+    V.wait_ge(S.lx, 16)
+    V.quantize_mx(T.xq[:], T.xs[:], T.xb[:]).then_inc(S.qx, 1)
+    V.wait_ge(S.la, 16)
+    V.quantize_mx(T.w1q[:, 0:128], T.w1s[:, 0:128], T.w1b[:, 0:512]).then_inc(S.qa, 1)
+    V.wait_ge(S.lb, 16)
+    V.quantize_mx(T.w1q[:, 128:256], T.w1s[:, 128:256], T.w1b[:, 512:1024]).then_inc(S.qb, 1)
+    PE.wait_ge(S.qx, 1)
+    PE.wait_ge(S.qa, 1)
+    PE.matmul_mx(T.z[:, 0:128], T.w1q[:, 0:128], T.w1s[:, 0:128], T.xq[:], T.xs[:], True, True).then_inc(S.m0, 1)
+    PE.wait_ge(S.qb, 1)
+    PE.matmul_mx(T.z[:, 512:640], T.w1q[:, 128:256], T.w1s[:, 128:256], T.xq[:], T.xs[:], True, True).then_inc(S.m1, 1)
+
+    SC.wait_ge(S.m0, 1)
+    SC.activation(T.sqj[:, 0:128], T.z[:, 0:128], A.Square, accum_out=T.l1[:, 4 * q:4 * q + 1]).then_inc(S.s0, 1)
+    SC.wait_ge(S.m1, 1)
+    SC.activation(T.sqj[:, 128:256], T.z[:, 512:640], A.Square, accum_out=T.l1[:, 4 * q + 1:4 * q + 2]).then_inc(S.s1, 1)
+
+    g.wait_ge(S.s0, 1)
+    g.wait_ge(S.s1, 1)
+    _spread(g, topo, core, peers, mine1, S.a1, S.out)
+
+    V.wait_ge(S.s0, 1)
+    V.tensor_scalar(T.pz[:, 0:128], T.z[:, 0:128], 0.0, None, OP.max).then_inc(S.pv, 1)
+    V.tensor_scalar(T.pz[:, 128:256], T.z[:, 0:128], -1.0, 0.0, OP.mult, OP.max).then_inc(S.pv, 1)
+    SC.activation(T.pz[:, 256:384], T.z[:, 512:640], A.Relu).then_inc(S.ps, 1)
+    SC.activation(T.pz[:, 384:512], T.z[:, 512:640], A.Relu, scale=-1.0).then_inc(S.ps, 1)
+
+    V.wait_ge(S.a1, in1)
+    V.tensor_reduce(T.l2[:, 4 * t:4 * t + 1], T.l1[:, 0:e1:4], axis=AxisListType.X, op=OP.add).then_inc(S.r0, 1)
+    SC.wait_ge(S.a1, in1)
+    SC.wait_ge(S.s1, 1)
+    SC.activation(T.j1[:, 0:len(groups[t])], T.l1[:, 1:e1:4], A.Copy, accum_out=T.l2[:, 4 * t + 1:4 * t + 2]).then_inc(S.r1, 1)
+
+    g.wait_ge(S.r0, 1)
+    g.wait_ge(S.r1, 1)
+    _spread(g, topo, core, fan[core], mine2, S.a2, S.out)
+
+    V.wait_ge(S.a2, in2)
+    V.wait_ge(S.r0, 1)
+    V.tensor_reduce(T.tot[:, 0:1], T.l2[:, 0:e2:4], axis=AxisListType.X, op=OP.add).then_inc(S.t0, 1)
+    SC.wait_ge(S.a2, in2)
+    SC.wait_ge(S.r1, 1)
+    SC.activation(T.j2[:, 0:len(groups)], T.l2[:, 1:e2:4], A.Copy, accum_out=T.tot[:, 1:2]).then_inc(S.t1, 1)
+
+    SC.wait_ge(S.t0, 1)
+    SC.wait_ge(S.t1, 1)
+    SC.activation(T.rt[:], T.tot[:], A.Sqrt, bias=EPS, scale=inv).then_inc(S.rs, 1)
+    V.wait_ge(S.t0, 1)
+    V.wait_ge(S.t1, 1)
+    V.tensor_scalar(T.vv[:], T.tot[:], inv, EPS, OP.mult, OP.add).then_inc(S.vs, 1)
+    V.wait_ge(S.vs, 1)
+    V.reciprocal(T.rv[:], T.vv[:]).then_inc(S.rc, 1)
+
+    V.wait_ge(S.rc, 1)
+    V.wait_ge(S.rs, 1)
+    V.wait_ge(S.pv, 2)
+    V.tensor_scalar(T.ht[:, 0:512:4], T.pz[:, 0:128], T.rt[:, 0:1], T.rv[:, 0:1], OP.mult, OP.mult).then_inc(S.hv, 1)
+    V.tensor_scalar(T.ht[:, 1:512:4], T.pz[:, 128:256], T.rt[:, 0:1], T.rv[:, 0:1], OP.mult, OP.mult).then_inc(S.hv, 1)
+    SC.wait_ge(S.rs, 1)
+    SC.wait_ge(S.rc, 1)
+    SC.activation(T.sf[:], T.rt[:, 1:2], A.Copy, scale=T.rv[:, 1:2]).then_inc(S.sc, 1)
+    SC.wait_ge(S.sc, 1)
+    SC.wait_ge(S.ps, 2)
+    SC.activation(T.ht[:, 2:512:4], T.pz[:, 256:384], A.Relu, scale=T.sf[:, 0:1]).then_inc(S.hc, 1)
+    SC.activation(T.ht[:, 3:512:4], T.pz[:, 384:512], A.Relu, scale=T.sf[:, 0:1]).then_inc(S.hc, 1)
+    V.wait_ge(S.hv, 2)
+    V.wait_ge(S.hc, 2)
+    V.quantize_mx(T.hq[:], T.hs[:], T.ht[:]).then_inc(S.qh, 1)
+
+    prev = cores[(rank - 1) % n]
+    nxt = cores[(rank + 1) % n]
+    rid, pid = topo.addr(prev, core)
+    m = topo.mask(core, prev)
+    g.wait_ge(S.qh, 1)
+    g.remote_dma(out_ap=T.nq[:].bitcast(dt.uint8), in_ap=T.hq[:].bitcast(dt.uint8), remote_sem=S.ah, local_sem=S.ho,
+                 pid=pid, routing_id=rid, dma_engine_mask=m)
+    g.remote_dma(out_ap=T.ns[:], in_ap=T.hs[:], remote_sem=S.ah, local_sem=S.ho, pid=pid, routing_id=rid, dma_engine_mask=m)
+
+    V.wait_ge(S.lw, 16)
+    V.quantize_mx(T.w2q[:], T.w2s[:], T.w2b[:]).then_inc(S.qw, 1)
+    PE.wait_ge(S.qh, 1)
+    PE.wait_ge(S.qw, 1)
+    PE.matmul_mx(T.yp[:, 0:128], T.w2q[:, 0:128], T.w2s[:, 0:128], T.hq[:], T.hs[:], True, False)
+    PE.wait_ge(S.ah, 2 * _engines(topo.mask(nxt, core)))
+    PE.matmul_mx(T.yp[:, 0:128], T.w2q[:, 128:256], T.w2s[:, 128:256], T.nq[:], T.ns[:], False, True).then_inc(S.my, 1)
+    V.wait_ge(S.my, 1)
+    V.tensor_copy(T.yb[:], T.yp[:, 0:128]).then_inc(S.yc, 1)
+
+    SY.wait_ge(S.hv, 2)
+    SY.wait_ge(S.hc, 2)
+    SY.wait_ge(S.ho, 2 * _engines(m))
+    SY.dma_start(T.h[:], T.ht[:]).then_inc(S.sh, 16)
+    SY.wait_ge(S.yc, 1)
+    SY.dma_start(T.y[:], T.yb[:]).then_inc(S.sy, 16)
+    SY.wait_ge(S.sh, 16)
+    SY.wait_ge(S.sy, 16)
+    g.wait_ge(S.out, _engines(_mask(topo, core, peers)) + _engines(_mask(topo, core, fan[core])))

@@ -3,6 +3,7 @@ from concourse.mybir import dt, AluOpType, AxisListType, ActivationFunctionType
 
 NC = 128
 EPS = 0.001
+OWN, PAD, FAR, TRI, END = 4, 6, 8, 6, 26
 
 SCRATCH = {
     "xb": ("sbuf", [128, 512], "bfloat16"),
@@ -16,18 +17,21 @@ SCRATCH = {
     "z": ("psum", [128, 1024], "float32"),
     "yp": ("psum", [128, 512], "float32"),
     "sqj": ("sbuf", [128, 256], "float32"),
-    "j1": ("sbuf", [128, 4], "float32"), "j2": ("sbuf", [128, 4], "float32"),
-    "l1": ("sbuf", [128, 12], "float32"),
-    "l2": ("sbuf", [128, 16], "float32"),
-    "tot": ("sbuf", [128, 2], "float32"),
-    "vv": ("sbuf", [128, 2], "float32"), "rv": ("sbuf", [128, 2], "float32"), "rt": ("sbuf", [128, 2], "float32"),
+    "L": ("sbuf", [128, END], "float32"),
+    "j2": ("sbuf", [128, 16], "float32"),
+    "vv": ("sbuf", [128, 2], "float32"), "qq": ("sbuf", [128, 2], "float32"), "cc": ("sbuf", [128, 2], "float32"),
+    "ro": ("sbuf", [128, 2], "float32"), "u0": ("sbuf", [128, 2], "float32"), "ua": ("sbuf", [128, 2], "float32"),
+    "ub": ("sbuf", [128, 2], "float32"), "uc": ("sbuf", [128, 2], "float32"), "u1": ("sbuf", [128, 2], "float32"),
+    "tot": ("sbuf", [128, 1], "float32"), "xx": ("sbuf", [128, 2], "float32"),
+    "rv": ("sbuf", [128, 2], "float32"), "rt": ("sbuf", [128, 2], "float32"),
     "sf": ("sbuf", [128, 1], "float32"),
     "pz": ("sbuf", [128, 512], "float32"),
     "ht": ("sbuf", [128, 512], "bfloat16"),
     "yb": ("sbuf", [128, 128], "float32"),
 }
-SEMAPHORES = ["lx", "la", "lb", "lw", "qx", "qa", "qb", "qw", "m0", "m1", "s0", "s1", "pv", "ps", "a1", "r0", "r1", "a2",
-              "t0", "t1", "rs", "vs", "rc", "sc", "hv", "hc", "qh", "ah", "my", "yc", "sh", "sy", "out", "ho"]
+SEMAPHORES = ["lx", "la", "lb", "lw", "qx", "qa", "qb", "qw", "m0", "m1", "s0", "s1", "pd", "pv", "ps", "a1", "a2",
+              "e1", "e2", "cs", "so", "n0", "n1", "n2", "n3", "up", "zv", "zs", "t0", "x0", "x1",
+              "rs", "rc", "sc", "hv", "hc", "qh", "ah", "my", "yc", "sh", "sy", "out", "ho"]
 
 
 def _plan(cores, topo):
@@ -61,13 +65,13 @@ def _engines(m):
     return bin(m).count("1")
 
 
-def _spread(g, topo, core, dsts, ap, remote_sem, local_sem):
+def _spread(g, topo, core, dsts, src, aps, remote_sem, local_sem):
     ids = []
     for d in dsts:
         rid, pid = topo.addr(d, core)
         ids.append(DstId(rid=rid, pnc=pid))
     g.remote_dma_fused([RemoteDMATransfer(dst_ids=ids, dma_engine_mask=_mask(topo, core, dsts), remote_sem=remote_sem,
-                                          srcs=[ap], dsts=[ap for _ in dsts], alu_op=0)], local_sem=local_sem)
+                                          srcs=[src], dsts=aps, alu_op=0)], local_sem=local_sem)
 
 
 def rank_program(g, core, T, topo):
@@ -77,22 +81,23 @@ def rank_program(g, core, T, topo):
     cores = [int(c) for c in T.cores]
     n = len(cores)
     groups, fan = _plan(cores, topo)
-    t = [i for i, gr in enumerate(groups) if core in gr][0]
-    q = groups[t].index(core)
-    peers = [u for u in groups[t] if u != core]
-    in1 = sum(_engines(_mask(topo, u, [w for w in groups[t] if w != u])) for u in peers)
-    in2 = sum(_engines(_mask(topo, u, fan[u])) for u in cores if core in fan[u])
+    others = {u: [w for w in gr if w != u] for gr in groups for u in gr}
+    heard = {v: [u for u in cores if v in fan[u]] for v in cores}
+    peers = others[core]
+    in1 = sum(_engines(_mask(topo, u, others[u])) for u in peers)
+    in2 = sum(_engines(_mask(topo, u, fan[u])) for u in heard[core])
     S, A, OP = T.sem, ActivationFunctionType, AluOpType
     V, SC, PE, SY = g.vector, g.scalar, g.tensor, g.sync
     inv = 1.0 / (n * NC)
-    mine1, mine2 = T.l1[:, 4 * q:4 * q + 2], T.l2[:, 4 * t:4 * t + 2]
-    e1 = len(groups[t]) * 4
-    e2 = len(groups) * 4
+    own = T.L[:, OWN:OWN + 2]
+    k = (END + 1) // 2
 
     SY.dma_start(T.xb[:], T.x[:]).then_inc(S.lx, 16)
     SC.dma_start(T.w1b[:, 0:512], T.w1[:, 0:512]).then_inc(S.la, 16)
     SY.dma_start(T.w1b[:, 512:1024], T.w1[:, 512:1024]).then_inc(S.lb, 16)
     SY.dma_start(T.w2b[:], T.w2[:]).then_inc(S.lw, 16)
+
+    V.memset(T.L[:, PAD:PAD + 2], EPS * n * NC).then_inc(S.pd, 1)
 
     V.wait_ge(S.lx, 16)
     V.quantize_mx(T.xq[:], T.xs[:], T.xb[:]).then_inc(S.qx, 1)
@@ -107,56 +112,82 @@ def rank_program(g, core, T, topo):
     PE.matmul_mx(T.z[:, 512:640], T.w1q[:, 128:256], T.w1s[:, 128:256], T.xq[:], T.xs[:], True, True).then_inc(S.m1, 1)
 
     SC.wait_ge(S.m0, 1)
-    SC.activation(T.sqj[:, 0:128], T.z[:, 0:128], A.Square, accum_out=T.l1[:, 4 * q:4 * q + 1]).then_inc(S.s0, 1)
+    SC.activation(T.sqj[:, 0:128], T.z[:, 0:128], A.Square, accum_out=T.L[:, OWN:OWN + 1]).then_inc(S.s0, 1)
     SC.wait_ge(S.m1, 1)
-    SC.activation(T.sqj[:, 128:256], T.z[:, 512:640], A.Square, accum_out=T.l1[:, 4 * q + 1:4 * q + 2]).then_inc(S.s1, 1)
+    SC.activation(T.sqj[:, 128:256], T.z[:, 512:640], A.Square, accum_out=T.L[:, OWN + 1:OWN + 2]).then_inc(S.s1, 1)
 
     g.wait_ge(S.s0, 1)
     g.wait_ge(S.s1, 1)
-    _spread(g, topo, core, peers, mine1, S.a1, S.out)
+    _spread(g, topo, core, peers, own, [T.L[:, 2 * others[d].index(core):2 * others[d].index(core) + 2] for d in peers],
+            S.a1, S.out)
+    g.wait_ge(S.a1, in1)
+    _spread(g, topo, core, fan[core], T.L[:, 0:TRI],
+            [T.L[:, FAR + TRI * heard[d].index(core):FAR + TRI * heard[d].index(core) + TRI] for d in fan[core]],
+            S.a2, S.out)
 
+    SC.wait_ge(S.s0, 1)
+    SC.wait_ge(S.s1, 1)
+    SC.activation(T.ro[:], own, A.Sqrt, bias=EPS, scale=inv).then_inc(S.so, 1)
+    SC.activation(T.pz[:, 256:384], T.z[:, 512:640], A.Relu).then_inc(S.ps, 1)
+    SC.activation(T.pz[:, 384:512], T.z[:, 512:640], A.Relu, scale=-1.0).then_inc(S.ps, 1)
     V.wait_ge(S.s0, 1)
     V.tensor_scalar(T.pz[:, 0:128], T.z[:, 0:128], 0.0, None, OP.max).then_inc(S.pv, 1)
     V.tensor_scalar(T.pz[:, 128:256], T.z[:, 0:128], -1.0, 0.0, OP.mult, OP.max).then_inc(S.pv, 1)
-    SC.activation(T.pz[:, 256:384], T.z[:, 512:640], A.Relu).then_inc(S.ps, 1)
-    SC.activation(T.pz[:, 384:512], T.z[:, 512:640], A.Relu, scale=-1.0).then_inc(S.ps, 1)
+    V.wait_ge(S.s1, 1)
+    V.tensor_scalar(T.vv[:], own, EPS * n * NC, inv, OP.add, OP.mult).then_inc(S.e1, 1)
+    V.wait_ge(S.e1, 1)
+    V.reciprocal(T.qq[:], T.vv[:]).then_inc(S.e2, 1)
+    V.wait_ge(S.e2, 1)
+    V.tensor_scalar(T.cc[:], T.qq[:], inv, None, OP.mult).then_inc(S.cs, 1)
+    V.wait_ge(S.so, 1)
+    V.tensor_tensor(T.u0[:], T.ro[:], T.qq[:], OP.mult).then_inc(S.n0, 1)
+    V.wait_ge(S.n0, 1)
+    V.tensor_tensor(T.ua[:], T.u0[:], T.u0[:], OP.mult).then_inc(S.n1, 1)
+    V.wait_ge(S.n1, 1)
+    V.tensor_tensor(T.ub[:], T.ua[:], T.vv[:], OP.mult).then_inc(S.n2, 1)
+    V.wait_ge(S.n2, 1)
+    V.tensor_scalar(T.uc[:], T.ub[:], -0.5, 1.5, OP.mult, OP.add).then_inc(S.n3, 1)
+    V.wait_ge(S.n3, 1)
+    V.tensor_tensor(T.u1[:], T.u0[:], T.uc[:], OP.mult).then_inc(S.up, 1)
+    V.wait_ge(S.up, 1)
+    V.wait_ge(S.pv, 2)
+    V.tensor_scalar(T.pz[:, 0:256], T.pz[:, 0:256], T.u1[:, 0:1], None, OP.mult).then_inc(S.zv, 1)
+    SC.wait_ge(S.up, 1)
+    SC.wait_ge(S.ps, 2)
+    SC.activation(T.pz[:, 256:512], T.pz[:, 256:512], A.Copy, scale=T.u1[:, 1:2]).then_inc(S.zs, 1)
+    V.wait_ge(S.lw, 16)
+    V.quantize_mx(T.w2q[:], T.w2s[:], T.w2b[:]).then_inc(S.qw, 1)
 
+    V.wait_ge(S.pd, 1)
     V.wait_ge(S.a1, in1)
-    V.tensor_reduce(T.l2[:, 4 * t:4 * t + 1], T.l1[:, 0:e1:4], axis=AxisListType.X, op=OP.add).then_inc(S.r0, 1)
-    SC.wait_ge(S.a1, in1)
-    SC.wait_ge(S.s1, 1)
-    SC.activation(T.j1[:, 0:len(groups[t])], T.l1[:, 1:e1:4], A.Copy, accum_out=T.l2[:, 4 * t + 1:4 * t + 2]).then_inc(S.r1, 1)
-
-    g.wait_ge(S.r0, 1)
-    g.wait_ge(S.r1, 1)
-    _spread(g, topo, core, fan[core], mine2, S.a2, S.out)
-
     V.wait_ge(S.a2, in2)
-    V.wait_ge(S.r0, 1)
-    V.tensor_reduce(T.tot[:, 0:1], T.l2[:, 0:e2:4], axis=AxisListType.X, op=OP.add).then_inc(S.t0, 1)
-    SC.wait_ge(S.a2, in2)
-    SC.wait_ge(S.r1, 1)
-    SC.activation(T.j2[:, 0:len(groups)], T.l2[:, 1:e2:4], A.Copy, accum_out=T.tot[:, 1:2]).then_inc(S.t1, 1)
-
-    SC.wait_ge(S.t0, 1)
-    SC.wait_ge(S.t1, 1)
-    SC.activation(T.rt[:], T.tot[:], A.Sqrt, bias=EPS, scale=inv).then_inc(S.rs, 1)
+    V.tensor_reduce(T.tot[:], T.L[:, 0:END:2], axis=AxisListType.X, op=OP.add).then_inc(S.t0, 1)
     V.wait_ge(S.t0, 1)
-    V.wait_ge(S.t1, 1)
-    V.tensor_scalar(T.vv[:], T.tot[:], inv, EPS, OP.mult, OP.add).then_inc(S.vs, 1)
-    V.wait_ge(S.vs, 1)
-    V.reciprocal(T.rv[:], T.vv[:]).then_inc(S.rc, 1)
+    V.wait_ge(S.cs, 1)
+    V.tensor_scalar(T.xx[:, 0:1], T.tot[:], T.cc[:, 0:1], None, OP.mult).then_inc(S.x0, 1)
+    SC.wait_ge(S.pd, 1)
+    SC.wait_ge(S.cs, 1)
+    SC.wait_ge(S.a1, in1)
+    SC.wait_ge(S.a2, in2)
+    SC.activation(T.j2[:, 0:k], T.L[:, 1:END:2], A.Copy, scale=T.cc[:, 1:2], accum_out=T.xx[:, 1:2]).then_inc(S.x1, 1)
+
+    SC.wait_ge(S.x0, 1)
+    SC.wait_ge(S.x1, 1)
+    SC.activation(T.rt[:], T.xx[:], A.Sqrt).then_inc(S.rs, 1)
+    V.wait_ge(S.x0, 1)
+    V.wait_ge(S.x1, 1)
+    V.reciprocal(T.rv[:], T.xx[:]).then_inc(S.rc, 1)
 
     V.wait_ge(S.rc, 1)
     V.wait_ge(S.rs, 1)
-    V.wait_ge(S.pv, 2)
+    V.wait_ge(S.zv, 1)
     V.tensor_scalar(T.ht[:, 0:512:4], T.pz[:, 0:128], T.rt[:, 0:1], T.rv[:, 0:1], OP.mult, OP.mult).then_inc(S.hv, 1)
     V.tensor_scalar(T.ht[:, 1:512:4], T.pz[:, 128:256], T.rt[:, 0:1], T.rv[:, 0:1], OP.mult, OP.mult).then_inc(S.hv, 1)
     SC.wait_ge(S.rs, 1)
     SC.wait_ge(S.rc, 1)
     SC.activation(T.sf[:], T.rt[:, 1:2], A.Copy, scale=T.rv[:, 1:2]).then_inc(S.sc, 1)
     SC.wait_ge(S.sc, 1)
-    SC.wait_ge(S.ps, 2)
+    SC.wait_ge(S.zs, 1)
     SC.activation(T.ht[:, 2:512:4], T.pz[:, 256:384], A.Relu, scale=T.sf[:, 0:1]).then_inc(S.hc, 1)
     SC.activation(T.ht[:, 3:512:4], T.pz[:, 384:512], A.Relu, scale=T.sf[:, 0:1]).then_inc(S.hc, 1)
     V.wait_ge(S.hv, 2)
@@ -172,8 +203,6 @@ def rank_program(g, core, T, topo):
                  pid=pid, routing_id=rid, dma_engine_mask=m)
     g.remote_dma(out_ap=T.ns[:], in_ap=T.hs[:], remote_sem=S.ah, local_sem=S.ho, pid=pid, routing_id=rid, dma_engine_mask=m)
 
-    V.wait_ge(S.lw, 16)
-    V.quantize_mx(T.w2q[:], T.w2s[:], T.w2b[:]).then_inc(S.qw, 1)
     PE.wait_ge(S.qh, 1)
     PE.wait_ge(S.qw, 1)
     PE.matmul_mx(T.yp[:, 0:128], T.w2q[:, 0:128], T.w2s[:, 0:128], T.hq[:], T.hs[:], True, False)

from concourse.bass import DstId, RemoteDMATransfer
from concourse.mybir import dt, AluOpType, AxisListType, ActivationFunctionType

NC = 128
EPS = 0.001
OWN, PAD, FAR, TRI, END = 4, 6, 8, 6, 26

SCRATCH = {
    "xb": ("sbuf", [128, 512], "bfloat16"),
    "w1b": ("sbuf", [128, 1024], "bfloat16"),
    "w2b": ("sbuf", [128, 1024], "bfloat16"),
    "xq": ("sbuf", [128, 128], "float8_e4m3fn_x4"), "xs": ("sbuf", [128, 128], "uint8"),
    "w1q": ("sbuf", [128, 256], "float8_e4m3fn_x4"), "w1s": ("sbuf", [128, 256], "uint8"),
    "w2q": ("sbuf", [128, 256], "float8_e4m3fn_x4"), "w2s": ("sbuf", [128, 256], "uint8"),
    "hq": ("sbuf", [128, 128], "float8_e4m3fn_x4"), "hs": ("sbuf", [128, 128], "uint8"),
    "nq": ("sbuf", [128, 128], "float8_e4m3fn_x4"), "ns": ("sbuf", [128, 128], "uint8"),
    "z": ("psum", [128, 1024], "float32"),
    "yp": ("psum", [128, 512], "float32"),
    "sqj": ("sbuf", [128, 256], "float32"),
    "L": ("sbuf", [128, END], "float32"),
    "j2": ("sbuf", [128, 16], "float32"),
    "vv": ("sbuf", [128, 2], "float32"), "qq": ("sbuf", [128, 2], "float32"), "cc": ("sbuf", [128, 2], "float32"),
    "ro": ("sbuf", [128, 2], "float32"), "u0": ("sbuf", [128, 2], "float32"), "ua": ("sbuf", [128, 2], "float32"),
    "ub": ("sbuf", [128, 2], "float32"), "uc": ("sbuf", [128, 2], "float32"), "u1": ("sbuf", [128, 2], "float32"),
    "tot": ("sbuf", [128, 1], "float32"), "xx": ("sbuf", [128, 2], "float32"),
    "rv": ("sbuf", [128, 2], "float32"), "rt": ("sbuf", [128, 2], "float32"),
    "sf": ("sbuf", [128, 1], "float32"),
    "pz": ("sbuf", [128, 512], "float32"),
    "ht": ("sbuf", [128, 512], "bfloat16"),
    "yb": ("sbuf", [128, 128], "float32"),
}
SEMAPHORES = ["lx", "la", "lb", "lw", "qx", "qa", "qb", "qw", "m0", "m1", "s0", "s1", "pd", "pv", "ps", "a1", "a2",
              "e1", "e2", "cs", "so", "n0", "n1", "n2", "n3", "up", "zv", "zs", "t0", "x0", "x1",
              "rs", "rc", "sc", "hv", "hc", "qh", "ah", "my", "yc", "sh", "sy", "out", "ho"]


def _plan(cores, topo):
    racks = {}
    for c in cores:
        racks.setdefault(topo.rack(topo.host(c)), {}).setdefault(topo.host(c), []).append(c)
    groups = []
    for rk in sorted(racks):
        a, b = [racks[rk][h] for h in sorted(racks[rk])]
        k = (len(a) + 1) // 2
        groups.append(a[:k] + b[:len(b) - k])
        groups.append(a[k:] + b[len(b) - k:])
    fan = {c: [] for c in cores}
    for gr in groups:
        rec = [v for v in cores if v not in gr]
        rec.sort(key=lambda v: sum(1 for u in gr if topo.may_write(u, v)))
        for v in rec:
            opts = [u for u in gr if topo.may_write(u, v)]
            fan[min(opts, key=lambda u: (len(fan[u]), topo.chip(u) != topo.chip(v)))].append(v)
    return groups, fan


def _mask(topo, src, dsts):
    m = topo.mask(src, dsts[0])
    for d in dsts[1:]:
        m &= topo.mask(src, d)
    return m


def _engines(m):
    return bin(m).count("1")


def _spread(g, topo, core, dsts, src, aps, remote_sem, local_sem):
    ids = []
    for d in dsts:
        rid, pid = topo.addr(d, core)
        ids.append(DstId(rid=rid, pnc=pid))
    g.remote_dma_fused([RemoteDMATransfer(dst_ids=ids, dma_engine_mask=_mask(topo, core, dsts), remote_sem=remote_sem,
                                          srcs=[src], dsts=aps, alu_op=0)], local_sem=local_sem)


def rank_program(g, core, T, topo):
    rank = T.rank_of(core)
    if rank is None:
        return
    cores = [int(c) for c in T.cores]
    n = len(cores)
    groups, fan = _plan(cores, topo)
    others = {u: [w for w in gr if w != u] for gr in groups for u in gr}
    heard = {v: [u for u in cores if v in fan[u]] for v in cores}
    peers = others[core]
    in1 = sum(_engines(_mask(topo, u, others[u])) for u in peers)
    in2 = sum(_engines(_mask(topo, u, fan[u])) for u in heard[core])
    S, A, OP = T.sem, ActivationFunctionType, AluOpType
    V, SC, PE, SY = g.vector, g.scalar, g.tensor, g.sync
    inv = 1.0 / (n * NC)
    own = T.L[:, OWN:OWN + 2]
    k = (END + 1) // 2

    SY.dma_start(T.xb[:], T.x[:]).then_inc(S.lx, 16)
    SC.dma_start(T.w1b[:, 0:512], T.w1[:, 0:512]).then_inc(S.la, 16)
    SY.dma_start(T.w1b[:, 512:1024], T.w1[:, 512:1024]).then_inc(S.lb, 16)
    SY.dma_start(T.w2b[:], T.w2[:]).then_inc(S.lw, 16)

    V.memset(T.L[:, PAD:PAD + 2], EPS * n * NC).then_inc(S.pd, 1)

    V.wait_ge(S.lx, 16)
    V.quantize_mx(T.xq[:], T.xs[:], T.xb[:]).then_inc(S.qx, 1)
    V.wait_ge(S.la, 16)
    V.quantize_mx(T.w1q[:, 0:128], T.w1s[:, 0:128], T.w1b[:, 0:512]).then_inc(S.qa, 1)
    V.wait_ge(S.lb, 16)
    V.quantize_mx(T.w1q[:, 128:256], T.w1s[:, 128:256], T.w1b[:, 512:1024]).then_inc(S.qb, 1)
    PE.wait_ge(S.qx, 1)
    PE.wait_ge(S.qa, 1)
    PE.matmul_mx(T.z[:, 0:128], T.w1q[:, 0:128], T.w1s[:, 0:128], T.xq[:], T.xs[:], True, True).then_inc(S.m0, 1)
    PE.wait_ge(S.qb, 1)
    PE.matmul_mx(T.z[:, 512:640], T.w1q[:, 128:256], T.w1s[:, 128:256], T.xq[:], T.xs[:], True, True).then_inc(S.m1, 1)

    SC.wait_ge(S.m0, 1)
    SC.activation(T.sqj[:, 0:128], T.z[:, 0:128], A.Square, accum_out=T.L[:, OWN:OWN + 1]).then_inc(S.s0, 1)
    SC.wait_ge(S.m1, 1)
    SC.activation(T.sqj[:, 128:256], T.z[:, 512:640], A.Square, accum_out=T.L[:, OWN + 1:OWN + 2]).then_inc(S.s1, 1)

    g.wait_ge(S.s0, 1)
    g.wait_ge(S.s1, 1)
    _spread(g, topo, core, peers, own, [T.L[:, 2 * others[d].index(core):2 * others[d].index(core) + 2] for d in peers],
            S.a1, S.out)
    g.wait_ge(S.a1, in1)
    _spread(g, topo, core, fan[core], T.L[:, 0:TRI],
            [T.L[:, FAR + TRI * heard[d].index(core):FAR + TRI * heard[d].index(core) + TRI] for d in fan[core]],
            S.a2, S.out)

    SC.wait_ge(S.s0, 1)
    SC.wait_ge(S.s1, 1)
    SC.activation(T.ro[:], own, A.Sqrt, bias=EPS, scale=inv).then_inc(S.so, 1)
    SC.activation(T.pz[:, 256:384], T.z[:, 512:640], A.Relu).then_inc(S.ps, 1)
    SC.activation(T.pz[:, 384:512], T.z[:, 512:640], A.Relu, scale=-1.0).then_inc(S.ps, 1)
    V.wait_ge(S.s0, 1)
    V.tensor_scalar(T.pz[:, 0:128], T.z[:, 0:128], 0.0, None, OP.max).then_inc(S.pv, 1)
    V.tensor_scalar(T.pz[:, 128:256], T.z[:, 0:128], -1.0, 0.0, OP.mult, OP.max).then_inc(S.pv, 1)
    V.wait_ge(S.s1, 1)
    V.tensor_scalar(T.vv[:], own, EPS * n * NC, inv, OP.add, OP.mult).then_inc(S.e1, 1)
    V.wait_ge(S.e1, 1)
    V.reciprocal(T.qq[:], T.vv[:]).then_inc(S.e2, 1)
    V.wait_ge(S.e2, 1)
    V.tensor_scalar(T.cc[:], T.qq[:], inv, None, OP.mult).then_inc(S.cs, 1)
    V.wait_ge(S.so, 1)
    V.tensor_tensor(T.u0[:], T.ro[:], T.qq[:], OP.mult).then_inc(S.n0, 1)
    V.wait_ge(S.n0, 1)
    V.tensor_tensor(T.ua[:], T.u0[:], T.u0[:], OP.mult).then_inc(S.n1, 1)
    V.wait_ge(S.n1, 1)
    V.tensor_tensor(T.ub[:], T.ua[:], T.vv[:], OP.mult).then_inc(S.n2, 1)
    V.wait_ge(S.n2, 1)
    V.tensor_scalar(T.uc[:], T.ub[:], -0.5, 1.5, OP.mult, OP.add).then_inc(S.n3, 1)
    V.wait_ge(S.n3, 1)
    V.tensor_tensor(T.u1[:], T.u0[:], T.uc[:], OP.mult).then_inc(S.up, 1)
    V.wait_ge(S.up, 1)
    V.wait_ge(S.pv, 2)
    V.tensor_scalar(T.pz[:, 0:256], T.pz[:, 0:256], T.u1[:, 0:1], None, OP.mult).then_inc(S.zv, 1)
    SC.wait_ge(S.up, 1)
    SC.wait_ge(S.ps, 2)
    SC.activation(T.pz[:, 256:512], T.pz[:, 256:512], A.Copy, scale=T.u1[:, 1:2]).then_inc(S.zs, 1)
    V.wait_ge(S.lw, 16)
    V.quantize_mx(T.w2q[:], T.w2s[:], T.w2b[:]).then_inc(S.qw, 1)

    V.wait_ge(S.pd, 1)
    V.wait_ge(S.a1, in1)
    V.wait_ge(S.a2, in2)
    V.tensor_reduce(T.tot[:], T.L[:, 0:END:2], axis=AxisListType.X, op=OP.add).then_inc(S.t0, 1)
    V.wait_ge(S.t0, 1)
    V.wait_ge(S.cs, 1)
    V.tensor_scalar(T.xx[:, 0:1], T.tot[:], T.cc[:, 0:1], None, OP.mult).then_inc(S.x0, 1)
    SC.wait_ge(S.pd, 1)
    SC.wait_ge(S.cs, 1)
    SC.wait_ge(S.a1, in1)
    SC.wait_ge(S.a2, in2)
    SC.activation(T.j2[:, 0:k], T.L[:, 1:END:2], A.Copy, scale=T.cc[:, 1:2], accum_out=T.xx[:, 1:2]).then_inc(S.x1, 1)

    SC.wait_ge(S.x0, 1)
    SC.wait_ge(S.x1, 1)
    SC.activation(T.rt[:], T.xx[:], A.Sqrt).then_inc(S.rs, 1)
    V.wait_ge(S.x0, 1)
    V.wait_ge(S.x1, 1)
    V.reciprocal(T.rv[:], T.xx[:]).then_inc(S.rc, 1)

    V.wait_ge(S.rc, 1)
    V.wait_ge(S.rs, 1)
    V.wait_ge(S.zv, 1)
    V.tensor_scalar(T.ht[:, 0:512:4], T.pz[:, 0:128], T.rt[:, 0:1], T.rv[:, 0:1], OP.mult, OP.mult).then_inc(S.hv, 1)
    V.tensor_scalar(T.ht[:, 1:512:4], T.pz[:, 128:256], T.rt[:, 0:1], T.rv[:, 0:1], OP.mult, OP.mult).then_inc(S.hv, 1)
    SC.wait_ge(S.rs, 1)
    SC.wait_ge(S.rc, 1)
    SC.activation(T.sf[:], T.rt[:, 1:2], A.Copy, scale=T.rv[:, 1:2]).then_inc(S.sc, 1)
    SC.wait_ge(S.sc, 1)
    SC.wait_ge(S.zs, 1)
    SC.activation(T.ht[:, 2:512:4], T.pz[:, 256:384], A.Relu, scale=T.sf[:, 0:1]).then_inc(S.hc, 1)
    SC.activation(T.ht[:, 3:512:4], T.pz[:, 384:512], A.Relu, scale=T.sf[:, 0:1]).then_inc(S.hc, 1)
    V.wait_ge(S.hv, 2)
    V.wait_ge(S.hc, 2)
    V.quantize_mx(T.hq[:], T.hs[:], T.ht[:]).then_inc(S.qh, 1)

    prev = cores[(rank - 1) % n]
    nxt = cores[(rank + 1) % n]
    rid, pid = topo.addr(prev, core)
    m = topo.mask(core, prev)
    g.wait_ge(S.qh, 1)
    g.remote_dma(out_ap=T.nq[:].bitcast(dt.uint8), in_ap=T.hq[:].bitcast(dt.uint8), remote_sem=S.ah, local_sem=S.ho,
                 pid=pid, routing_id=rid, dma_engine_mask=m)
    g.remote_dma(out_ap=T.ns[:], in_ap=T.hs[:], remote_sem=S.ah, local_sem=S.ho, pid=pid, routing_id=rid, dma_engine_mask=m)

    PE.wait_ge(S.qh, 1)
    PE.wait_ge(S.qw, 1)
    PE.matmul_mx(T.yp[:, 0:128], T.w2q[:, 0:128], T.w2s[:, 0:128], T.hq[:], T.hs[:], True, False)
    PE.wait_ge(S.ah, 2 * _engines(topo.mask(nxt, core)))
    PE.matmul_mx(T.yp[:, 0:128], T.w2q[:, 128:256], T.w2s[:, 128:256], T.nq[:], T.ns[:], False, True).then_inc(S.my, 1)
    V.wait_ge(S.my, 1)
    V.tensor_copy(T.yb[:], T.yp[:, 0:128]).then_inc(S.yc, 1)

    SY.wait_ge(S.hv, 2)
    SY.wait_ge(S.hc, 2)
    SY.wait_ge(S.ho, 2 * _engines(m))
    SY.dma_start(T.h[:], T.ht[:]).then_inc(S.sh, 16)
    SY.wait_ge(S.yc, 1)
    SY.dma_start(T.y[:], T.yb[:]).then_inc(S.sy, 16)
    SY.wait_ge(S.sh, 16)
    SY.wait_ge(S.sy, 16)
    g.wait_ge(S.out, _engines(_mask(topo, core, peers)) + _engines(_mask(topo, core, fan[core])))
